import numpy as np
import ml_dtypes


def mxq(x, axis, fmt="e4m3"):
    dtype, down = {"e4m3": (ml_dtypes.float8_e4m3fn, 7), "e5m2": (ml_dtypes.float8_e5m2, 14)}[fmt]
    v = np.moveaxis(np.asarray(x, np.float32).astype(ml_dtypes.bfloat16).astype(np.float64), axis, -1)
    blocks = v.reshape(v.shape[:-1] + (-1, 32))
    amax = np.abs(blocks).max(-1, keepdims=True)
    byte = np.maximum(np.where(amax > 0, np.frexp(amax)[1] - 1 + 127, 0) - down, 1)
    scale = np.exp2(byte - 127.0)
    codes = (blocks / scale).astype(np.float32).astype(dtype).astype(np.float64)
    return np.moveaxis((codes * scale).reshape(v.shape), -1, axis)


WIDE = False


def mx_kscale(k, group=512):
    if not WIDE:
        return np.ones(k)
    levels = np.array([18, -18])
    if group != 512:
        return np.exp2(np.random.permutation(np.resize(levels, k // group))).repeat(group)
    if k % 512:
        return np.exp2(np.random.permutation(np.resize(levels, k // 32))).repeat(32)
    a = np.empty((k // 512, 16))
    for p in range(k // 512):
        a[p, :8] = np.random.permutation(np.resize(levels, 8))
        for g in range(8):
            far = levels[np.abs(levels - a[p, g]) >= 10]
            a[p, g + 8] = far[np.random.randint(len(far))]
    return np.exp2(a.ravel()).repeat(32)


def f64(x):
    return np.asarray(x).astype(np.float64)


G, D, M, N = 4, 128, 128, 512


def setup_inputs():
    n = np.random.standard_normal
    s_d = mx_kscale(D, 0)
    return {
        "h": (n((G, D, N)) * s_d[:, None]).astype(np.float32),
        "ws": (n((G, D, M)) / np.sqrt(D) / s_d[:, None]).astype(np.float32),
        "y0": (n((G, M, N))).astype(np.float32),
        "sh": (n((G, M, N))).astype(np.float32),
    }


def reference(h, ws, y0, sh):
    wsq = mxq(f64(ws), 1, "e4m3")
    hq = mxq(f64(h), 1, "e4m3")
    zs = wsq.transpose(0, 2, 1) @ hq
    y = f64(y0) * (1.0 + np.tanh(zs)) + f64(sh)
    return y

@@ -1,0 +1,126 @@
+from contextlib import ExitStack
+
+import concourse.mybir as mybir
+
+G, D, M, N = 4, 128, 128, 512
+FLOPS = 2 * G * D * M * N
+
+F32 = mybir.dt.float32
+BF16 = mybir.dt.bfloat16
+U32 = mybir.dt.uint32
+U8 = mybir.dt.uint8
+FP8X4 = mybir.dt.float8_e4m3fn_x4
+ACT = mybir.ActivationFunctionType
+ALU = mybir.AluOpType
+
+P = 128
+PACK = 4
+ROWS = D // PACK
+COLS = 128
+HALF = 256
+RUN = 4
+
+
+def walk(raw, packed):
+    src = raw.rearrange("p j (c i) -> p c j i", i=RUN)
+    dst = packed.rearrange("p (c i) j -> p c j i", i=RUN)
+    return src, dst
+
+
+def pack_on_vector(nc, raw, packed):
+    src, dst = walk(raw, packed)
+    nc.vector.tensor_copy(out=dst, in_=src)
+
+
+def pack_on_scalar(nc, raw, packed):
+    src, dst = walk(raw, packed)
+    nc.scalar.activation(out=dst, in_=src, func=ACT.Copy)
+
+
+def quantize(nc, packed, codes, scales):
+    nc.vector.quantize_mx(
+        out=codes[:].bitcast(FP8X4),
+        scales=scales[:],
+        in_=packed[:].rearrange("p c j -> p (c j)"),
+    )
+
+
+def tile_rows_cell_film_kernel(tc, h, ws, y0, sh, out):
+    nc = tc.nc
+    chunks = N // COLS
+    halves = N // HALF
+    per_half = HALF // COLS
+
+    with ExitStack() as ctx:
+        sb = ctx.enter_context(tc.tile_pool(name="sb", bufs=1))
+        ps = ctx.enter_context(tc.psum_pool(name="ps", bufs=1))
+        ctx.enter_context(tc.manual_schedule())
+
+        w_raw = sb.tile([P, PACK, M], F32, name="w_raw")
+        h_raw = sb.tile([P, PACK, N], F32, name="h_raw")
+        y_in = [sb.tile([M, N], F32, name="y_in%d" % g) for g in range(G)]
+        s_in = [sb.tile([M, N], F32, name="s_in%d" % g) for g in range(G)]
+        res = [sb.tile([M, N], F32, name="res%d" % g) for g in range(G)]
+
+        w_packed = sb.tile([P, M, PACK], BF16, name="w_packed", align_bytes=64)
+        w_codes = sb.tile([P, M], U32, name="w_codes", align_bytes=64)
+        w_scales = sb.tile([P, M], U8, name="w_scales", align_bytes=64)
+        h_packed = [sb.tile([P, COLS, PACK], BF16, name="h_packed%d" % c, align_bytes=64) for c in range(chunks)]
+        h_codes = [sb.tile([P, COLS], U32, name="h_codes%d" % c, align_bytes=64) for c in range(chunks)]
+        h_scales = [sb.tile([P, COLS], U8, name="h_scales%d" % c, align_bytes=64) for c in range(chunks)]
+
+        units = [(g, u) for g in range(G) for u in range(halves)]
+        zs = {gu: ps.tile([M, HALF], F32, name="zs%d_%d" % gu) for gu in units}
+        gate = {gu: sb.tile([M, HALF], F32, name="gate%d_%d" % gu) for gu in units}
+        scaled = {gu: sb.tile([M, HALF], F32, name="scaled%d_%d" % gu) for gu in units}
+
+        nc.sync.dma_start(out=w_raw[:], in_=ws.rearrange("g (p j) m -> (g p) j m", j=PACK))
+        nc.sync.dma_start(out=h_raw[:], in_=h.rearrange("g (p j) n -> (g p) j n", j=PACK))
+        for g in range(G):
+            nc.sync.dma_start(out=y_in[g][:], in_=y0[g])
+            nc.sync.dma_start(out=s_in[g][:], in_=sh[g])
+
+        pack_on_scalar(nc, w_raw[:], w_packed[:])
+        quantize(nc, w_packed, w_codes, w_scales)
+
+        for c in range(chunks):
+            cols = slice(c * COLS, (c + 1) * COLS)
+            pack = pack_on_vector if c < per_half else pack_on_scalar
+            pack(nc, h_raw[:, :, cols], h_packed[c][:])
+
+        for c in range(chunks):
+            quantize(nc, h_packed[c], h_codes[c], h_scales[c])
+            u, place = divmod(c, per_half)
+            for g in range(G):
+                rows = slice(g * ROWS, (g + 1) * ROWS)
+                nc.tensor.matmul_mx(
+                    out=zs[(g, u)][:, place * COLS:(place + 1) * COLS],
+                    lhsT=w_codes[rows, :].bitcast(FP8X4),
+                    lhsT_scale=w_scales[rows, :],
+                    rhs=h_codes[c][rows, :].bitcast(FP8X4),
+                    rhs_scale=h_scales[c][rows, :],
+                    start=True,
+                    stop=True,
+                )
+
+        def modulate(g, u):
+            cols = slice(u * HALF, (u + 1) * HALF)
+            nc.scalar.activation(out=gate[(g, u)][:], in_=zs[(g, u)][:], func=ACT.Tanh)
+            nc.vector.scalar_tensor_tensor(
+                out=scaled[(g, u)][:], in0=gate[(g, u)][:], scalar=1.0, in1=y_in[g][:, cols],
+                op0=ALU.add, op1=ALU.mult,
+            )
+
+        def shift(g, u):
+            cols = slice(u * HALF, (u + 1) * HALF)
+            nc.vector.tensor_tensor(out=res[g][:, cols], in0=scaled[(g, u)][:], in1=s_in[g][:, cols], op=ALU.add)
+            if g == G - 1:
+                nc.sync.dma_start(out=out[g][:, cols], in_=res[g][:, cols])
+            elif u == halves - 1:
+                nc.sync.dma_start(out=out[g], in_=res[g][:])
+
+        for i, gu in enumerate(units):
+            modulate(*gu)
+            if i > 0:
+                shift(*units[i - 1])
+        shift(*units[-1])

@@ -88,20 +88,25 @@ def tile_rows_cell_film_kernel(tc, h, ws, y0, sh, out):
             pack = pack_on_vector if c < per_half else pack_on_scalar
             pack(nc, h_raw[:, :, cols], h_packed[c][:])
 
+        def multiply(g, c):
+            rows = slice(g * ROWS, (g + 1) * ROWS)
+            u, place = divmod(c, per_half)
+            nc.tensor.matmul_mx(
+                out=zs[(g, u)][:, place * COLS:(place + 1) * COLS],
+                lhsT=w_codes[rows, :].bitcast(FP8X4),
+                lhsT_scale=w_scales[rows, :],
+                rhs=h_codes[c][rows, :].bitcast(FP8X4),
+                rhs_scale=h_scales[c][rows, :],
+                start=True,
+                stop=True,
+            )
+
         for c in range(chunks):
             quantize(nc, h_packed[c], h_codes[c], h_scales[c])
-            u, place = divmod(c, per_half)
-            for g in range(G):
-                rows = slice(g * ROWS, (g + 1) * ROWS)
-                nc.tensor.matmul_mx(
-                    out=zs[(g, u)][:, place * COLS:(place + 1) * COLS],
-                    lhsT=w_codes[rows, :].bitcast(FP8X4),
-                    lhsT_scale=w_scales[rows, :],
-                    rhs=h_codes[c][rows, :].bitcast(FP8X4),
-                    rhs_scale=h_scales[c][rows, :],
-                    start=True,
-                    stop=True,
-                )
+        for first in range(0, G, 2):
+            for c in range(chunks):
+                for g in (first, first + 1):
+                    multiply(g, c)
 
         def modulate(g, u):
             cols = slice(u * HALF, (u + 1) * HALF)

@@ -18,23 +18,15 @@ PACK = 4
 ROWS = D // PACK
 COLS = 128
 HALF = 256
-RUN = 4
-
-
-def walk(raw, packed):
-    src = raw.rearrange("p j (c i) -> p c j i", i=RUN)
-    dst = packed.rearrange("p (c i) j -> p c j i", i=RUN)
-    return src, dst
+PAIR = 2
 
 
 def pack_on_vector(nc, raw, packed):
-    src, dst = walk(raw, packed)
-    nc.vector.tensor_copy(out=dst, in_=src)
+    nc.vector.tensor_copy(out=packed, in_=raw.rearrange("p j c -> p c j"))
 
 
 def pack_on_scalar(nc, raw, packed):
-    src, dst = walk(raw, packed)
-    nc.scalar.activation(out=dst, in_=src, func=ACT.Copy)
+    nc.scalar.activation(out=packed, in_=raw.rearrange("p j c -> p c j"), func=ACT.Copy)
 
 
 def quantize(nc, packed, codes, scales):
@@ -57,7 +49,7 @@ def tile_rows_cell_film_kernel(tc, h, ws, y0, sh, out):
         ctx.enter_context(tc.manual_schedule())
 
         w_raw = sb.tile([P, PACK, M], F32, name="w_raw")
-        h_raw = sb.tile([P, PACK, N], F32, name="h_raw")
+        h_raw = [sb.tile([P, PAIR, N], F32, name="h_raw%d" % t) for t in range(PACK // PAIR)]
         y_in = [sb.tile([M, N], F32, name="y_in%d" % g) for g in range(G)]
         s_in = [sb.tile([M, N], F32, name="s_in%d" % g) for g in range(G)]
         res = [sb.tile([M, N], F32, name="res%d" % g) for g in range(G)]
@@ -75,7 +67,9 @@ def tile_rows_cell_film_kernel(tc, h, ws, y0, sh, out):
         scaled = {gu: sb.tile([M, HALF], F32, name="scaled%d_%d" % gu) for gu in units}
 
         nc.sync.dma_start(out=w_raw[:], in_=ws.rearrange("g (p j) m -> (g p) j m", j=PACK))
-        nc.sync.dma_start(out=h_raw[:], in_=h.rearrange("g (p j) n -> (g p) j n", j=PACK))
+        h_rows = h.rearrange("g (p j) n -> (g p) j n", j=PACK)
+        for t in range(PACK // PAIR):
+            nc.sync.dma_start(out=h_raw[t][:], in_=h_rows[:, t * PAIR:(t + 1) * PAIR, :])
         for g in range(G):
             nc.sync.dma_start(out=y_in[g][:], in_=y0[g])
             nc.sync.dma_start(out=s_in[g][:], in_=sh[g])
@@ -83,10 +77,11 @@ def tile_rows_cell_film_kernel(tc, h, ws, y0, sh, out):
         pack_on_scalar(nc, w_raw[:], w_packed[:])
         quantize(nc, w_packed, w_codes, w_scales)
 
-        for c in range(chunks):
-            cols = slice(c * COLS, (c + 1) * COLS)
-            pack = pack_on_vector if c < per_half else pack_on_scalar
-            pack(nc, h_raw[:, :, cols], h_packed[c][:])
+        for t in range(PACK // PAIR):
+            for c in range(chunks):
+                cols = slice(c * COLS, (c + 1) * COLS)
+                pack = pack_on_vector if c < per_half else pack_on_scalar
+                pack(nc, h_raw[t][:, :, cols], h_packed[c][:, :, t * PAIR:(t + 1) * PAIR])
 
         def multiply(g, c):
             rows = slice(g * ROWS, (g + 1) * ROWS)

@@ -61,10 +61,18 @@ def tile_rows_cell_film_kernel(tc, h, ws, y0, sh, out):
         h_codes = [sb.tile([P, COLS], U32, name="h_codes%d" % c, align_bytes=64) for c in range(chunks)]
         h_scales = [sb.tile([P, COLS], U8, name="h_scales%d" % c, align_bytes=64) for c in range(chunks)]
 
-        units = [(g, u) for g in range(G) for u in range(halves)]
-        zs = {gu: ps.tile([M, HALF], F32, name="zs%d_%d" % gu) for gu in units}
-        gate = {gu: sb.tile([M, HALF], F32, name="gate%d_%d" % gu) for gu in units}
-        scaled = {gu: sb.tile([M, HALF], F32, name="scaled%d_%d" % gu) for gu in units}
+        units = [(0, c * COLS, COLS) for c in range(chunks)]
+        units = units + [(g, u * HALF, HALF) for g in range(1, G) for u in range(halves)]
+        zs = {}
+        for c in range(chunks):
+            bank = ps.tile([M, COLS], F32, name="bank0_%d" % c)
+            zs[(0, c * COLS)] = bank[:]
+        for g in range(1, G):
+            bank = ps.tile([M, N], F32, name="bank%d" % g)
+            for c in range(chunks):
+                zs[(g, c * COLS)] = bank[:, c * COLS:]
+        gate = {unit: sb.tile([M, unit[2]], F32, name="gate%d_%d" % unit[:2]) for unit in units}
+        scaled = {unit: sb.tile([M, unit[2]], F32, name="scaled%d_%d" % unit[:2]) for unit in units}
 
         nc.sync.dma_start(out=w_raw[:], in_=ws.rearrange("g (p j) m -> (g p) j m", j=PACK))
         h_rows = h.rearrange("g (p j) n -> (g p) j n", j=PACK)
@@ -85,9 +93,8 @@ def tile_rows_cell_film_kernel(tc, h, ws, y0, sh, out):
 
         def multiply(g, c):
             rows = slice(g * ROWS, (g + 1) * ROWS)
-            u, place = divmod(c, per_half)
             nc.tensor.matmul_mx(
-                out=zs[(g, u)][:, place * COLS:(place + 1) * COLS],
+                out=zs[(g, c * COLS)][:, :COLS],
                 lhsT=w_codes[rows, :].bitcast(FP8X4),
                 lhsT_scale=w_scales[rows, :],
                 rhs=h_codes[c][rows, :].bitcast(FP8X4),
@@ -103,24 +110,25 @@ def tile_rows_cell_film_kernel(tc, h, ws, y0, sh, out):
                 for g in (first, first + 1):
                     multiply(g, c)
 
-        def modulate(g, u):
-            cols = slice(u * HALF, (u + 1) * HALF)
-            nc.scalar.activation(out=gate[(g, u)][:], in_=zs[(g, u)][:], func=ACT.Tanh)
+        def modulate(unit):
+            g, start, width = unit
+            nc.scalar.activation(out=gate[unit][:], in_=zs[(g, start)][:, :width], func=ACT.Tanh)
             nc.vector.scalar_tensor_tensor(
-                out=scaled[(g, u)][:], in0=gate[(g, u)][:], scalar=1.0, in1=y_in[g][:, cols],
+                out=scaled[unit][:], in0=gate[unit][:], scalar=1.0, in1=y_in[g][:, start:start + width],
                 op0=ALU.add, op1=ALU.mult,
             )
 
-        def shift(g, u):
-            cols = slice(u * HALF, (u + 1) * HALF)
-            nc.vector.tensor_tensor(out=res[g][:, cols], in0=scaled[(g, u)][:], in1=s_in[g][:, cols], op=ALU.add)
+        def shift(unit):
+            g, start, width = unit
+            cols = slice(start, start + width)
+            nc.vector.tensor_tensor(out=res[g][:, cols], in0=scaled[unit][:], in1=s_in[g][:, cols], op=ALU.add)
             if g == G - 1:
                 nc.sync.dma_start(out=out[g][:, cols], in_=res[g][:, cols])
-            elif u == halves - 1:
+            elif start + width == N:
                 nc.sync.dma_start(out=out[g], in_=res[g][:])
 
-        for i, gu in enumerate(units):
-            modulate(*gu)
+        for i, unit in enumerate(units):
+            modulate(unit)
             if i > 0:
-                shift(*units[i - 1])
-        shift(*units[-1])
+                shift(units[i - 1])
+        shift(units[-1])

from contextlib import ExitStack

import concourse.mybir as mybir

G, D, M, N = 4, 128, 128, 512
FLOPS = 2 * G * D * M * N

F32 = mybir.dt.float32
BF16 = mybir.dt.bfloat16
U32 = mybir.dt.uint32
U8 = mybir.dt.uint8
FP8X4 = mybir.dt.float8_e4m3fn_x4
ACT = mybir.ActivationFunctionType
ALU = mybir.AluOpType

P = 128
PACK = 4
ROWS = D // PACK
COLS = 128
HALF = 256
PAIR = 2


def pack_on_vector(nc, raw, packed):
    nc.vector.tensor_copy(out=packed, in_=raw.rearrange("p j c -> p c j"))


def pack_on_scalar(nc, raw, packed):
    nc.scalar.activation(out=packed, in_=raw.rearrange("p j c -> p c j"), func=ACT.Copy)


def quantize(nc, packed, codes, scales):
    nc.vector.quantize_mx(
        out=codes[:].bitcast(FP8X4),
        scales=scales[:],
        in_=packed[:].rearrange("p c j -> p (c j)"),
    )


def tile_rows_cell_film_kernel(tc, h, ws, y0, sh, out):
    nc = tc.nc
    chunks = N // COLS
    halves = N // HALF
    per_half = HALF // COLS

    with ExitStack() as ctx:
        sb = ctx.enter_context(tc.tile_pool(name="sb", bufs=1))
        ps = ctx.enter_context(tc.psum_pool(name="ps", bufs=1))
        ctx.enter_context(tc.manual_schedule())

        w_raw = sb.tile([P, PACK, M], F32, name="w_raw")
        h_raw = [sb.tile([P, PAIR, N], F32, name="h_raw%d" % t) for t in range(PACK // PAIR)]
        y_in = [sb.tile([M, N], F32, name="y_in%d" % g) for g in range(G)]
        s_in = [sb.tile([M, N], F32, name="s_in%d" % g) for g in range(G)]
        res = [sb.tile([M, N], F32, name="res%d" % g) for g in range(G)]

        w_packed = sb.tile([P, M, PACK], BF16, name="w_packed", align_bytes=64)
        w_codes = sb.tile([P, M], U32, name="w_codes", align_bytes=64)
        w_scales = sb.tile([P, M], U8, name="w_scales", align_bytes=64)
        h_packed = [sb.tile([P, COLS, PACK], BF16, name="h_packed%d" % c, align_bytes=64) for c in range(chunks)]
        h_codes = [sb.tile([P, COLS], U32, name="h_codes%d" % c, align_bytes=64) for c in range(chunks)]
        h_scales = [sb.tile([P, COLS], U8, name="h_scales%d" % c, align_bytes=64) for c in range(chunks)]

        units = [(0, c * COLS, COLS) for c in range(chunks)]
        units = units + [(g, u * HALF, HALF) for g in range(1, G) for u in range(halves)]
        zs = {}
        for c in range(chunks):
            bank = ps.tile([M, COLS], F32, name="bank0_%d" % c)
            zs[(0, c * COLS)] = bank[:]
        for g in range(1, G):
            bank = ps.tile([M, N], F32, name="bank%d" % g)
            for c in range(chunks):
                zs[(g, c * COLS)] = bank[:, c * COLS:]
        gate = {unit: sb.tile([M, unit[2]], F32, name="gate%d_%d" % unit[:2]) for unit in units}
        scaled = {unit: sb.tile([M, unit[2]], F32, name="scaled%d_%d" % unit[:2]) for unit in units}

        nc.sync.dma_start(out=w_raw[:], in_=ws.rearrange("g (p j) m -> (g p) j m", j=PACK))
        h_rows = h.rearrange("g (p j) n -> (g p) j n", j=PACK)
        for t in range(PACK // PAIR):
            nc.sync.dma_start(out=h_raw[t][:], in_=h_rows[:, t * PAIR:(t + 1) * PAIR, :])
        for g in range(G):
            nc.sync.dma_start(out=y_in[g][:], in_=y0[g])
            nc.sync.dma_start(out=s_in[g][:], in_=sh[g])

        pack_on_scalar(nc, w_raw[:], w_packed[:])
        quantize(nc, w_packed, w_codes, w_scales)

        for t in range(PACK // PAIR):
            for c in range(chunks):
                cols = slice(c * COLS, (c + 1) * COLS)
                pack = pack_on_vector if c < per_half else pack_on_scalar
                pack(nc, h_raw[t][:, :, cols], h_packed[c][:, :, t * PAIR:(t + 1) * PAIR])

        def multiply(g, c):
            rows = slice(g * ROWS, (g + 1) * ROWS)
            nc.tensor.matmul_mx(
                out=zs[(g, c * COLS)][:, :COLS],
                lhsT=w_codes[rows, :].bitcast(FP8X4),
                lhsT_scale=w_scales[rows, :],
                rhs=h_codes[c][rows, :].bitcast(FP8X4),
                rhs_scale=h_scales[c][rows, :],
                start=True,
                stop=True,
            )

        for c in range(chunks):
            quantize(nc, h_packed[c], h_codes[c], h_scales[c])
        for first in range(0, G, 2):
            for c in range(chunks):
                for g in (first, first + 1):
                    multiply(g, c)

        def modulate(unit):
            g, start, width = unit
            nc.scalar.activation(out=gate[unit][:], in_=zs[(g, start)][:, :width], func=ACT.Tanh)
            nc.vector.scalar_tensor_tensor(
                out=scaled[unit][:], in0=gate[unit][:], scalar=1.0, in1=y_in[g][:, start:start + width],
                op0=ALU.add, op1=ALU.mult,
            )

        def shift(unit):
            g, start, width = unit
            cols = slice(start, start + width)
            nc.vector.tensor_tensor(out=res[g][:, cols], in0=scaled[unit][:], in1=s_in[g][:, cols], op=ALU.add)
            if g == G - 1:
                nc.sync.dma_start(out=out[g][:, cols], in_=res[g][:, cols])
            elif start + width == N:
                nc.sync.dma_start(out=out[g], in_=res[g][:])

        for i, unit in enumerate(units):
            modulate(unit)
            if i > 0:
                shift(units[i - 1])
        shift(units[-1])
